import numpy as np
import ml_dtypes


def mxq(x, axis, fmt="e4m3"):
    dtype, down = {"e4m3": (ml_dtypes.float8_e4m3fn, 7), "e5m2": (ml_dtypes.float8_e5m2, 14)}[fmt]
    v = np.moveaxis(np.asarray(x, np.float32).astype(ml_dtypes.bfloat16).astype(np.float64), axis, -1)
    blocks = v.reshape(v.shape[:-1] + (-1, 32))
    amax = np.abs(blocks).max(-1, keepdims=True)
    byte = np.maximum(np.where(amax > 0, np.frexp(amax)[1] - 1 + 127, 0) - down, 1)
    scale = np.exp2(byte - 127.0)
    codes = (blocks / scale).astype(np.float32).astype(dtype).astype(np.float64)
    return np.moveaxis((codes * scale).reshape(v.shape), -1, axis)


WIDE = False


def mx_kscale(k):
    if not WIDE:
        return np.ones(k)
    levels = np.array([10, -10, 5, -5, 0])
    if k % 512:
        return np.exp2(np.random.permutation(np.resize(levels, k // 32))).repeat(32)
    a = np.empty((k // 512, 16))
    for p in range(k // 512):
        a[p, :8] = np.random.permutation(np.resize(levels, 8))
        for g in range(8):
            far = levels[np.abs(levels - a[p, g]) >= 10]
            a[p, g + 8] = far[np.random.randint(len(far))]
    return np.exp2(a.ravel()).repeat(32)


def f64(x):
    return np.asarray(x).astype(np.float64)


def striped(idx):
    return np.tile(idx.reshape(-1, 16).T, (8, 1)).astype(np.uint16)


def unstriped(offs):
    return offs[:16].T.reshape(-1).astype(np.int64)


def pack_weight(w):
    k, n = w.shape
    w = f64(np.asarray(w, np.float32).astype(ml_dtypes.bfloat16)).reshape(k // 32, 32, n)
    amax = np.abs(w).max(1)
    byte = np.clip(np.where(amax > 0, np.frexp(amax)[1] - 1 + 127 - 7, 1), 1, 254)
    scaled = (w * np.exp2(127.0 - byte)[:, None, :]).reshape(k, n).astype(np.float32)
    words = np.ascontiguousarray(scaled.reshape(k // 512, 128, 4, n).transpose(0, 1, 3, 2)).astype(ml_dtypes.float8_e4m3fn).view(np.uint8)
    return words, np.ascontiguousarray(byte.astype(np.uint8).reshape(k // 512, 16, n))


def unpack_weight(words, scales):
    g, p, n, _ = words.shape
    vals = np.ascontiguousarray(words).view(ml_dtypes.float8_e4m3fn).astype(np.float64) * np.repeat(np.exp2(scales.astype(np.float64) - 127.0), 8, axis=1)[..., None]
    return vals.transpose(0, 1, 3, 2).reshape(g * 512, n)


def planes(y):
    n, m = y.shape
    v = y.astype(np.float32).astype(ml_dtypes.bfloat16).astype(np.float64).reshape(n // 32, 32, m)
    top = np.abs(v).max(1)
    byte = np.clip(np.where(top > 0, np.frexp(top)[1] - 1 + 127 - 7, 1), 1, 254)
    codes = (v * np.exp2(127.0 - byte)[:, None, :]).reshape(n, m).astype(np.float32).astype(ml_dtypes.float8_e4m3fn).view(np.uint8)
    words = codes.reshape(n // 512, 128, 4, m).transpose(0, 1, 3, 2)
    return np.ascontiguousarray(words), np.ascontiguousarray(byte.astype(np.uint8).reshape(n // 512, 16, m))


K, T, S, H, N = 512, 2048, 512, 512, 512


def setup_inputs():
    n = np.random.standard_normal
    s = mx_kscale(K)[:, None]
    u = mx_kscale(H)
    packed_xT = pack_weight(n((K, T)) * s)
    return {
        "x_words": packed_xT[0],
        "x_scales": packed_xT[1],
        "w1": (n((K, N)) / np.sqrt(K) / s).astype(np.float32),
        "unit": (np.random.uniform(0.5, 1.5, (H, 1)) * u[:, None]).astype(np.float32),
        "wx": (n((H, 1))).astype(np.float32),
        "wt": (n((H, 1))).astype(np.float32),
        "w2": (n((H, N)) / np.sqrt(H) / u[:, None]).astype(np.float32),
        "offs": striped(np.random.permutation(T)[:S]),
    }


def reference(x_words, x_scales, w1, unit, wx, wt, w2, offs):
    xq = unpack_weight(x_words, x_scales)[:, unstriped(offs)]
    h = np.tanh(mxq(f64(w1), 0, "e4m3").T @ xq)
    h1 = -1.0 * ((h) ** 2) + 1.0
    zut = f64(unit) * (f64(wt) * h1)
    w2q = mxq(f64(w2), 0, "e4m3")
    ut = w2q.T @ mxq(zut, 0, "e4m3")
    zu0 = f64(unit) * h
    u0 = w2q.T @ mxq(zu0, 0, "e4m3")
    zux = f64(unit) * (f64(wx) * h1)
    ux = w2q.T @ mxq(zux, 0, "e4m3")
    zuxx = f64(unit) * (f64(wx) * (f64(wx) * (-2.0 * (h * h1))))
    uxx = w2q.T @ mxq(zuxx, 0, "e4m3")
    out_0 = ut + u0 * ux - (0.3 * uxx)
    return (out_0,) + planes(out_0)

@@ -1,0 +1,315 @@
+from contextlib import ExitStack
+
+import concourse.mybir as mybir
+
+K, T, S, H, N = 512, 2048, 512, 512, 512
+FLOPS = 5 * 2 * 512 * 512 * 512
+
+F32 = mybir.dt.float32
+BF16 = mybir.dt.bfloat16
+I32 = mybir.dt.int32
+U32 = mybir.dt.uint32
+U16 = mybir.dt.uint16
+U8 = mybir.dt.uint8
+FP8X4 = mybir.dt.float8_e4m3fn_x4
+ACT = mybir.ActivationFunctionType
+MULT, ADD = mybir.AluOpType.mult, mybir.AluOpType.add
+
+P = 128
+PACK = 4
+CHUNK = 256
+UNIT = 128
+M_SPLIT = 84
+U0, UX, UT, UXX = 0, 1, 2, 3
+
+
+def deal_weight(engine_copy, grouped, raw, m0, m1):
+    engine_copy(
+        grouped[:].rearrange("p (t m r) -> p m r t", t=PACK, r=PACK)[:, m0:m1],
+        raw[:].rearrange("p r (m t) -> p m r t", t=PACK)[:, m0:m1],
+    )
+
+
+def interleave(engine_copy, grouped, slots):
+    engine_copy(
+        grouped.rearrange("p (c i t) -> p c t i", t=PACK, i=4),
+        slots.rearrange("p t (c i) -> p c t i", i=4),
+    )
+
+
+def tile_picked_ypinn_burg_po_kernel(
+    tc, x_words, x_scales, w1, unit, wx, wt, w2, offs, out_0, out_1, out_2
+):
+    nc = tc.nc
+    with ExitStack() as ctx:
+        keep = ctx.enter_context(tc.tile_pool(name="keep", bufs=1))
+        work = ctx.enter_context(tc.tile_pool(name="work", bufs=2))
+        psum = ctx.enter_context(tc.psum_pool(name="psum", bufs=8))
+
+        def affine(on_scalar, out, in_, scale, bias):
+            if on_scalar:
+                if bias is None:
+                    nc.scalar.activation(out, in_, ACT.Copy, scale=scale)
+                else:
+                    nc.scalar.activation(out, in_, ACT.Identity, bias=bias, scale=scale)
+            elif bias is None:
+                nc.vector.tensor_scalar(out, in_, scale, None, MULT)
+            else:
+                nc.vector.tensor_scalar(out, in_, scale, bias, MULT, ADD)
+
+        scale_table = keep.tile([P, T], U8, align_bytes=64)
+        nc.gpsimd.memset(scale_table[:].bitcast(I32), 0)
+        warm = keep.tile([P, 1], F32)
+        warm_out = keep.tile([P, 1], F32)
+        nc.gpsimd.memset(warm[:], 0.0)
+
+        w1_raw = keep.tile([P, PACK, H], F32)
+        nc.sync.dma_start(w1_raw[:], w1.rearrange("(p r) c -> p r c", r=PACK))
+        offsets = keep.tile([P, S // 16], U16)
+        nc.sync.dma_start(offsets[:], offs)
+        for q in range(4):
+            nc.scalar.dma_start(
+                scale_table[32 * q : 32 * q + 4, :].bitcast(I32),
+                x_scales[0, 4 * q : 4 * q + 4, :].bitcast(I32),
+            )
+        nc.scalar.activation(warm_out[:], warm[:], ACT.Tanh)
+        word_table = keep.tile([P, T], U32, align_bytes=64)
+        nc.sync.dma_start(
+            word_table[:].bitcast(I32), x_words[0].rearrange("p n t -> p (n t)").bitcast(I32)
+        )
+        unit_c = keep.tile([P, PACK], F32)
+        wx_c = keep.tile([P, PACK], F32)
+        wt_c = keep.tile([P, PACK], F32)
+        for column, vec in ((unit_c, unit), (wx_c, wx), (wt_c, wt)):
+            nc.gpsimd.dma_start(column[:], vec.rearrange("(p t) o -> p (t o)", t=PACK))
+        w2_raw = keep.tile([P, PACK, N], F32)
+        nc.sync.dma_start(w2_raw[:], w2.rearrange("(p r) c -> p r c", r=PACK))
+
+        w1_bf = keep.tile([P, PACK * H], BF16, align_bytes=64)
+        w1_codes = keep.tile([P, H], U32, align_bytes=64)
+        w1_scales = keep.tile([P, H], U8, align_bytes=64)
+        deal_weight(nc.vector.tensor_copy, w1_bf, w1_raw, 0, M_SPLIT)
+        deal_weight(nc.scalar.copy, w1_bf, w1_raw, M_SPLIT, P)
+
+        x_codes, x_bytes = [], []
+        for c in range(S // CHUNK):
+            picked = keep.tile([P, CHUNK], U8, align_bytes=64, name=f"x_bytes{c}")
+            lst = offsets[:, c * CHUNK // 16 : (c + 1) * CHUNK // 16]
+            nc.vector.tensor_copy(picked[:], scale_table[:].indirect(lst))
+            x_bytes.append(picked)
+        nc.vector.quantize_mx(w1_codes[:].bitcast(FP8X4), w1_scales[:], w1_bf[:])
+
+        c_ut = keep.tile([P, PACK], F32)
+        c_ux = keep.tile([P, PACK], F32)
+        neg_ut = keep.tile([P, PACK], F32)
+        neg_ux = keep.tile([P, PACK], F32)
+        c_xx = keep.tile([P, PACK], F32)
+        nc.gpsimd.tensor_tensor(c_ut[:], unit_c[:], wt_c[:], MULT)
+        nc.gpsimd.tensor_tensor(c_ux[:], unit_c[:], wx_c[:], MULT)
+        nc.gpsimd.tensor_scalar(neg_ut[:], c_ut[:], -1.0, 0.0, MULT, ADD)
+        nc.gpsimd.tensor_scalar(neg_ux[:], c_ux[:], -1.0, 0.0, MULT, ADD)
+        nc.gpsimd.tensor_scalar(c_xx[:], wx_c[:], -2.0, 0.0, MULT, ADD)
+
+        for c in range(S // CHUNK):
+            picked = keep.tile([P, CHUNK], U32, align_bytes=64, name=f"x_codes{c}")
+            lst = offsets[:, c * CHUNK // 16 : (c + 1) * CHUNK // 16]
+            nc.vector.tensor_copy(picked[:], word_table[:].indirect(lst))
+            x_codes.append(picked)
+
+        def hidden(c):
+            h = keep.tile([P, PACK, CHUNK], F32, name=f"h{c}")
+            sq = keep.tile([P, PACK, CHUNK], F32, name=f"sq{c}")
+            for pair in range(2):
+                bank = psum.tile([P, 2, CHUNK], F32, name="bank")
+                for e in range(2):
+                    t = 2 * pair + e
+                    nc.tensor.matmul_mx(
+                        bank[:, e, :],
+                        lhsT=w1_codes[:, t * P : (t + 1) * P].bitcast(FP8X4),
+                        lhsT_scale=w1_scales[:, t * P : (t + 1) * P],
+                        rhs=x_codes[c][:].bitcast(FP8X4),
+                        rhs_scale=x_bytes[c][:],
+                        start=True,
+                        stop=True,
+                    )
+                nc.scalar.activation(h[:, 2 * pair : 2 * pair + 2, :], bank[:], ACT.Tanh)
+            for pair in range(2):
+                ts = slice(2 * pair, 2 * pair + 2)
+                nc.scalar.activation(sq[:, ts, :], h[:, ts, :], ACT.Square)
+            return h, sq
+
+        y_codes = keep.tile([P, S], U32, align_bytes=64)
+        y_scales = keep.tile([P, S], U8, align_bytes=64)
+        out_rows = out_0.rearrange("(p t) j -> p t j", t=PACK)
+        out_words = out_1[0].rearrange("p n t -> p (n t)").bitcast(I32)
+        w2_bf = keep.tile([P, PACK * N], BF16, align_bytes=64)
+        w2_codes = keep.tile([P, N], U32, align_bytes=64)
+        w2_scales = keep.tile([P, N], U8, align_bytes=64)
+
+        units = range(S // UNIT)
+        z = {}
+        grouped = {}
+        packed = {}
+        banks = {}
+        stage = {}
+        for u in units:
+            for half in range(2):
+                grouped[u, half] = keep.tile(
+                    [P, 2, PACK * UNIT], BF16, align_bytes=64, name=f"grouped{u}_{half}"
+                )
+                packed[u, half] = (
+                    keep.tile([P, 2 * UNIT], U32, align_bytes=64, name=f"codes{u}_{half}"),
+                    keep.tile([P, 2 * UNIT], U8, align_bytes=64, name=f"scales{u}_{half}"),
+                )
+
+        def scaled(kind, c, on_scalar):
+            h, sq = hid[c]
+            src, scale, bias, dtype = {
+                U0: (h, unit_c, None, BF16),
+                UX: (sq, neg_ux, c_ux, F32),
+                UT: (sq, neg_ut, c_ut, BF16),
+            }[kind]
+            z[kind, c] = keep.tile([P, PACK, CHUNK], dtype, name=f"z{kind}_{c}")
+            for t in range(PACK):
+                col = slice(t, t + 1)
+                affine(
+                    on_scalar, z[kind, c][:, t, :], src[:, t, :], scale[:, col],
+                    None if bias is None else bias[:, col],
+                )
+
+        def second(c):
+            h, sq = hid[c]
+            z[UXX, c] = keep.tile([P, PACK, CHUNK], BF16, name=f"z{UXX}_{c}")
+            for t in range(PACK):
+                nc.vector.scalar_tensor_tensor(
+                    z[UXX, c][:, t, :], h[:, t, :], c_xx[:, t : t + 1], z[UX, c][:, t, :], MULT, MULT
+                )
+
+        def weave(kind, u, engine_copy):
+            c, lo = divmod(u * UNIT, CHUNK)
+            interleave(engine_copy, grouped[u, kind // 2][:, kind % 2, :], z[kind, c][:, :, lo : lo + UNIT])
+
+        def heads(u, half):
+            codes, scales = packed[u, half]
+            nc.vector.quantize_mx(
+                codes[:].bitcast(FP8X4), scales[:], grouped[u, half][:].rearrange("p k c -> p (k c)")
+            )
+            for e in range(2):
+                bank = psum.tile([P, PACK, UNIT], F32, name="bank")
+                for t in range(PACK):
+                    nc.tensor.matmul_mx(
+                        bank[:, t, :],
+                        lhsT=w2_codes[:, t * P : (t + 1) * P].bitcast(FP8X4),
+                        lhsT_scale=w2_scales[:, t * P : (t + 1) * P],
+                        rhs=codes[:, e * UNIT : (e + 1) * UNIT].bitcast(FP8X4),
+                        rhs_scale=scales[:, e * UNIT : (e + 1) * UNIT],
+                        start=True,
+                        stop=True,
+                    )
+                banks[2 * half + e, u] = bank
+
+        def fetch_u0(u):
+            stage[u] = work.tile([P, PACK, UNIT], F32, name="u0_sb")
+            nc.scalar.copy(stage[u][:], banks[U0, u][:])
+
+        def times_ux(u):
+            prod = work.tile([P, PACK, UNIT], F32, name="prod")
+            nc.vector.tensor_tensor(prod[:], banks[UX, u][:], stage[u][:], MULT)
+            stage[u] = prod
+
+        def plus_ut(u):
+            part = work.tile([P, PACK, UNIT], F32, name="part")
+            nc.vector.tensor_tensor(part[:], banks[UT, u][:], stage[u][:], ADD)
+            stage[u] = part
+
+        def minus_uxx(u):
+            y = keep.tile([P, PACK, UNIT], F32, name=f"y{u}")
+            nc.vector.scalar_tensor_tensor(
+                y[:].rearrange("p t j -> p (t j)"),
+                banks[UXX, u][:].rearrange("p t j -> p (t j)"),
+                -0.3,
+                stage[u][:].rearrange("p t j -> p (t j)"),
+                MULT,
+                ADD,
+            )
+            nc.sync.dma_start(out_rows[:, :, u * UNIT : (u + 1) * UNIT], y[:])
+            stage[u] = y
+
+        def round_y(u, engine_copy):
+            y_bf = work.tile([P, PACK * UNIT], BF16, align_bytes=64, name="y_bf")
+            interleave(engine_copy, y_bf[:], stage[u][:])
+            stage[u] = y_bf
+
+        def pack_y(u):
+            cols = slice(u * UNIT, (u + 1) * UNIT)
+            nc.vector.quantize_mx(y_codes[:, cols].bitcast(FP8X4), y_scales[:, cols], stage[u][:])
+            nc.sync.dma_start(out_words[:, cols], y_codes[:, cols].bitcast(I32))
+
+        vcopy, scopy = nc.vector.tensor_copy, nc.scalar.copy
+        hid = {}
+        hid[0] = hidden(0)
+        scaled(U0, 0, False)
+        scaled(UX, 0, True)
+        scaled(UT, 0, True)
+        hid[1] = hidden(1)
+        weave(U0, 0, vcopy)
+        weave(U0, 1, vcopy)
+        deal_weight(vcopy, w2_bf, w2_raw, 0, P)
+        weave(UX, 0, vcopy)
+        nc.vector.quantize_mx(w2_codes[:].bitcast(FP8X4), w2_scales[:], w2_bf[:])
+        second(0)
+        heads(0, 0)
+        fetch_u0(0)
+        scaled(UX, 1, True)
+        scaled(U0, 1, True)
+        weave(UT, 0, vcopy)
+        weave(UXX, 0, vcopy)
+        weave(UX, 1, vcopy)
+        heads(0, 1)
+        weave(UT, 1, vcopy)
+        heads(1, 0)
+        fetch_u0(1)
+        scaled(UT, 1, True)
+        weave(UXX, 1, vcopy)
+        times_ux(0)
+        heads(1, 1)
+        plus_ut(0)
+        second(1)
+        minus_uxx(0)
+        round_y(0, scopy)
+        weave(UX, 2, vcopy)
+        times_ux(1)
+        weave(U0, 2, vcopy)
+        weave(UT, 2, scopy)
+        plus_ut(1)
+        heads(2, 0)
+        fetch_u0(2)
+        weave(U0, 3, scopy)
+        weave(UX, 3, scopy)
+        weave(UXX, 2, vcopy)
+        minus_uxx(1)
+        heads(2, 1)
+        weave(UT, 3, scopy)
+        weave(UXX, 3, scopy)
+        pack_y(0)
+        times_ux(2)
+        heads(3, 0)
+        fetch_u0(3)
+        round_y(1, scopy)
+        plus_ut(2)
+        heads(3, 1)
+        minus_uxx(2)
+        round_y(2, scopy)
+        times_ux(3)
+        pack_y(1)
+        plus_ut(3)
+        pack_y(2)
+        minus_uxx(3)
+        round_y(3, vcopy)
+        pack_y(3)
+        for q in range(4):
+            queue = nc.sync if q % 2 == 0 else nc.scalar
+            queue.dma_start(
+                out_2[0, 4 * q : 4 * q + 4, :].bitcast(I32),
+                y_scales[32 * q : 32 * q + 4, :].bitcast(I32),
+            )

@@ -19,22 +19,27 @@ P = 128
 PACK = 4
 CHUNK = 256
 UNIT = 128
-M_SPLIT = 84
-U0, UX, UT, UXX = 0, 1, 2, 3
+M_SPLIT = 48
+U0, UX, UT, UXX, HC = 0, 1, 2, 3, 4
 
 
-def deal_weight(engine_copy, grouped, raw, m0, m1):
+def deal_weight(engine_copy, grouped, raw, m0, m1, first=0):
     engine_copy(
         grouped[:].rearrange("p (t m r) -> p m r t", t=PACK, r=PACK)[:, m0:m1],
-        raw[:].rearrange("p r (m t) -> p m r t", t=PACK)[:, m0:m1],
+        raw[:].rearrange("p r (m t) -> p m r t", t=PACK)[:, m0 - first : m1 - first],
     )
+
+
+def woven(grouped):
+    return grouped.rearrange("p (c i t) -> p c t i", t=PACK, i=4)
+
+
+def slotted(slots):
+    return slots.rearrange("p t (c i) -> p c t i", i=4)
 
 
 def interleave(engine_copy, grouped, slots):
-    engine_copy(
-        grouped.rearrange("p (c i t) -> p c t i", t=PACK, i=4),
-        slots.rearrange("p t (c i) -> p c t i", i=4),
-    )
+    engine_copy(woven(grouped), slotted(slots))
 
 
 def tile_picked_ypinn_burg_po_kernel(
@@ -46,44 +51,50 @@ def tile_picked_ypinn_burg_po_kernel(
         work = ctx.enter_context(tc.tile_pool(name="work", bufs=2))
         psum = ctx.enter_context(tc.psum_pool(name="psum", bufs=8))
 
-        def affine(on_scalar, out, in_, scale, bias):
-            if on_scalar:
+        def affine(engine, out, in_, scale, bias):
+            if engine is nc.scalar:
                 if bias is None:
                     nc.scalar.activation(out, in_, ACT.Copy, scale=scale)
                 else:
                     nc.scalar.activation(out, in_, ACT.Identity, bias=bias, scale=scale)
-            elif bias is None:
-                nc.vector.tensor_scalar(out, in_, scale, None, MULT)
             else:
-                nc.vector.tensor_scalar(out, in_, scale, bias, MULT, ADD)
+                engine.tensor_scalar(out, in_, scale, zero[:] if bias is None else bias, MULT, ADD)
 
+        unit_c = keep.tile([P, PACK], F32)
+        wx_c = keep.tile([P, PACK], F32)
+        wt_c = keep.tile([P, PACK], F32)
         scale_table = keep.tile([P, T], U8, align_bytes=64)
-        nc.gpsimd.memset(scale_table[:].bitcast(I32), 0)
-        warm = keep.tile([P, 1], F32)
-        warm_out = keep.tile([P, 1], F32)
-        nc.gpsimd.memset(warm[:], 0.0)
+        nc.vector.memset(scale_table[:].bitcast(I32), 0)
+        warm = keep.tile([P, 1], F32, tag="words", align_bytes=64)
+        warm_mid = keep.tile([P, 1], F32, tag="w2_0")
+        warm_out = keep.tile([P, 1], F32, tag="w2_1")
+        nc.vector.memset(warm[:], 0.0)
+        zero = keep.tile([P, 1], F32)
+        nc.vector.tensor_copy(zero[:], warm[:])
+        for column, vec in ((unit_c, unit), (wx_c, wx), (wt_c, wt)):
+            nc.gpsimd.dma_start(column[:], vec.rearrange("(p t) o -> p (t o)", t=PACK))
 
         w1_raw = keep.tile([P, PACK, H], F32)
         nc.sync.dma_start(w1_raw[:], w1.rearrange("(p r) c -> p r c", r=PACK))
         offsets = keep.tile([P, S // 16], U16)
         nc.sync.dma_start(offsets[:], offs)
         for q in range(4):
-            nc.scalar.dma_start(
+            nc.sync.dma_start(
                 scale_table[32 * q : 32 * q + 4, :].bitcast(I32),
                 x_scales[0, 4 * q : 4 * q + 4, :].bitcast(I32),
             )
-        nc.scalar.activation(warm_out[:], warm[:], ACT.Tanh)
-        word_table = keep.tile([P, T], U32, align_bytes=64)
+        nc.scalar.activation(warm_mid[:], zero[:], ACT.Tanh)
+        nc.scalar.activation(warm_out[:], warm_mid[:], ACT.Square)
+        word_table = keep.tile([P, T], U32, tag="words", align_bytes=64)
         nc.sync.dma_start(
             word_table[:].bitcast(I32), x_words[0].rearrange("p n t -> p (n t)").bitcast(I32)
         )
-        unit_c = keep.tile([P, PACK], F32)
-        wx_c = keep.tile([P, PACK], F32)
-        wt_c = keep.tile([P, PACK], F32)
-        for column, vec in ((unit_c, unit), (wx_c, wx), (wt_c, wt)):
-            nc.gpsimd.dma_start(column[:], vec.rearrange("(p t) o -> p (t o)", t=PACK))
-        w2_raw = keep.tile([P, PACK, N], F32)
-        nc.sync.dma_start(w2_raw[:], w2.rearrange("(p r) c -> p r c", r=PACK))
+        w2_raw = []
+        for half in range(2):
+            raw = keep.tile([P, PACK, N // 2], F32, tag=f"w2_{half}", name=f"w2_raw{half}")
+            cols = slice(half * N // 2, (half + 1) * N // 2)
+            nc.sync.dma_start(raw[:], w2.rearrange("(p r) c -> p r c", r=PACK)[:, :, cols])
+            w2_raw.append(raw)
 
         w1_bf = keep.tile([P, PACK * H], BF16, align_bytes=64)
         w1_codes = keep.tile([P, H], U32, align_bytes=64)
@@ -104,11 +115,11 @@ def tile_picked_ypinn_burg_po_kernel(
         neg_ut = keep.tile([P, PACK], F32)
         neg_ux = keep.tile([P, PACK], F32)
         c_xx = keep.tile([P, PACK], F32)
-        nc.gpsimd.tensor_tensor(c_ut[:], unit_c[:], wt_c[:], MULT)
         nc.gpsimd.tensor_tensor(c_ux[:], unit_c[:], wx_c[:], MULT)
-        nc.gpsimd.tensor_scalar(neg_ut[:], c_ut[:], -1.0, 0.0, MULT, ADD)
         nc.gpsimd.tensor_scalar(neg_ux[:], c_ux[:], -1.0, 0.0, MULT, ADD)
         nc.gpsimd.tensor_scalar(c_xx[:], wx_c[:], -2.0, 0.0, MULT, ADD)
+        nc.gpsimd.tensor_tensor(c_ut[:], unit_c[:], wt_c[:], MULT)
+        nc.gpsimd.tensor_scalar(neg_ut[:], c_ut[:], -1.0, 0.0, MULT, ADD)
 
         for c in range(S // CHUNK):
             picked = keep.tile([P, CHUNK], U32, align_bytes=64, name=f"x_codes{c}")
@@ -116,9 +127,9 @@ def tile_picked_ypinn_burg_po_kernel(
             nc.vector.tensor_copy(picked[:], word_table[:].indirect(lst))
             x_codes.append(picked)
 
-        def hidden(c):
-            h = keep.tile([P, PACK, CHUNK], F32, name=f"h{c}")
-            sq = keep.tile([P, PACK, CHUNK], F32, name=f"sq{c}")
+        pre, hid, squares = {}, {}, {}
+
+        def first_layer(c):
             for pair in range(2):
                 bank = psum.tile([P, 2, CHUNK], F32, name="bank")
                 for e in range(2):
@@ -132,11 +143,18 @@ def tile_picked_ypinn_burg_po_kernel(
                         start=True,
                         stop=True,
                     )
-                nc.scalar.activation(h[:, 2 * pair : 2 * pair + 2, :], bank[:], ACT.Tanh)
+                pre[c, pair] = bank
+
+        def tanh(c):
+            hid[c] = keep.tile([P, PACK, CHUNK], F32, name=f"h{c}")
+            for pair in range(2):
+                nc.scalar.activation(hid[c][:, 2 * pair : 2 * pair + 2, :], pre[c, pair][:], ACT.Tanh)
+
+        def square(c):
+            squares[c] = keep.tile([P, PACK, CHUNK], F32, name=f"sq{c}")
             for pair in range(2):
                 ts = slice(2 * pair, 2 * pair + 2)
-                nc.scalar.activation(sq[:, ts, :], h[:, ts, :], ACT.Square)
-            return h, sq
+                nc.scalar.activation(squares[c][:, ts, :], hid[c][:, ts, :], ACT.Square)
 
         y_codes = keep.tile([P, S], U32, align_bytes=64)
         y_scales = keep.tile([P, S], U8, align_bytes=64)
@@ -146,55 +164,71 @@ def tile_picked_ypinn_burg_po_kernel(
         w2_codes = keep.tile([P, N], U32, align_bytes=64)
         w2_scales = keep.tile([P, N], U8, align_bytes=64)
 
-        units = range(S // UNIT)
         z = {}
         grouped = {}
         packed = {}
         banks = {}
         stage = {}
-        for u in units:
-            for half in range(2):
-                grouped[u, half] = keep.tile(
-                    [P, 2, PACK * UNIT], BF16, align_bytes=64, name=f"grouped{u}_{half}"
-                )
-                packed[u, half] = (
-                    keep.tile([P, 2 * UNIT], U32, align_bytes=64, name=f"codes{u}_{half}"),
-                    keep.tile([P, 2 * UNIT], U8, align_bytes=64, name=f"scales{u}_{half}"),
-                )
+        side = {}
+        def pair_up(*members):
+            name = "_".join(f"{kind}{u}" for kind, u in members)
+            wide = keep.tile([P, 2, PACK * UNIT], BF16, align_bytes=64, name=f"grouped{name}")
+            packed[members] = (
+                wide,
+                keep.tile([P, 2 * UNIT], U32, align_bytes=64, name=f"codes{name}"),
+                keep.tile([P, 2 * UNIT], U8, align_bytes=64, name=f"scales{name}"),
+            )
+            for e, member in enumerate(members):
+                grouped[member] = wide[:, e, :]
 
-        def scaled(kind, c, on_scalar):
-            h, sq = hid[c]
+        pair_up((U0, 0), (U0, 1))
+        pair_up((UX, 0), (UX, 1))
+        pair_up((UT, 0), (UT, 1))
+        pair_up((UXX, 0), (UXX, 1))
+        pair_up((U0, 2), (U0, 3))
+        pair_up((UX, 2), (UX, 3))
+        pair_up((UT, 2), (UXX, 2))
+        pair_up((UT, 3), (UXX, 3))
+
+        def of_unit(tiles, u):
+            c, lo = divmod(u * UNIT, CHUNK)
+            return tiles[c][:, :, lo : lo + UNIT]
+
+        def scaled(kind, first, count, engine, tag):
+            c, lo = divmod(first * UNIT, CHUNK)
             src, scale, bias, dtype = {
-                U0: (h, unit_c, None, BF16),
-                UX: (sq, neg_ux, c_ux, F32),
-                UT: (sq, neg_ut, c_ut, BF16),
+                U0: (hid, unit_c, None, BF16),
+                HC: (hid, c_xx, None, F32),
+                UX: (squares, neg_ux, c_ux, F32),
+                UT: (squares, neg_ut, c_ut, BF16),
             }[kind]
-            z[kind, c] = keep.tile([P, PACK, CHUNK], dtype, name=f"z{kind}_{c}")
+            slots = keep.tile([P, PACK, count * UNIT], dtype, name=f"z{kind}_{first}", tag=tag)
             for t in range(PACK):
                 col = slice(t, t + 1)
                 affine(
-                    on_scalar, z[kind, c][:, t, :], src[:, t, :], scale[:, col],
+                    engine, slots[:, t, :], src[c][:, t, lo : lo + count * UNIT], scale[:, col],
                     None if bias is None else bias[:, col],
                 )
+            for n in range(count):
+                z[kind, first + n] = slots[:, :, n * UNIT : (n + 1) * UNIT]
 
-        def second(c):
-            h, sq = hid[c]
-            z[UXX, c] = keep.tile([P, PACK, CHUNK], BF16, name=f"z{UXX}_{c}")
-            for t in range(PACK):
-                nc.vector.scalar_tensor_tensor(
-                    z[UXX, c][:, t, :], h[:, t, :], c_xx[:, t : t + 1], z[UX, c][:, t, :], MULT, MULT
-                )
+        def target(kind, u):
+            return grouped[kind, u]
 
         def weave(kind, u, engine_copy):
-            c, lo = divmod(u * UNIT, CHUNK)
-            interleave(engine_copy, grouped[u, kind // 2][:, kind % 2, :], z[kind, c][:, :, lo : lo + UNIT])
+            interleave(engine_copy, target(kind, u), z[kind, u])
 
-        def heads(u, half):
-            codes, scales = packed[u, half]
-            nc.vector.quantize_mx(
-                codes[:].bitcast(FP8X4), scales[:], grouped[u, half][:].rearrange("p k c -> p (k c)")
-            )
-            for e in range(2):
+        def direct_u0(u):
+            spread = unit_c[:].unsqueeze(1).unsqueeze(3).to_broadcast([P, UNIT // 4, PACK, 4])
+            nc.vector.tensor_tensor(woven(target(U0, u)), slotted(of_unit(hid, u)), spread, MULT)
+
+        def direct_uxx(u):
+            nc.vector.tensor_tensor(woven(target(UXX, u)), slotted(z[HC, u]), slotted(z[UX, u]), MULT)
+
+        def heads(*members):
+            wide, codes, scales = packed[members]
+            nc.vector.quantize_mx(codes[:].bitcast(FP8X4), scales[:], wide[:].rearrange("p k c -> p (k c)"))
+            for e, member in enumerate(members):
                 bank = psum.tile([P, PACK, UNIT], F32, name="bank")
                 for t in range(PACK):
                     nc.tensor.matmul_mx(
@@ -206,7 +240,7 @@ def tile_picked_ypinn_burg_po_kernel(
                         start=True,
                         stop=True,
                     )
-                banks[2 * half + e, u] = bank
+                banks[member] = bank
 
         def fetch_u0(u):
             stage[u] = work.tile([P, PACK, UNIT], F32, name="u0_sb")
@@ -235,6 +269,28 @@ def tile_picked_ypinn_burg_po_kernel(
             nc.sync.dma_start(out_rows[:, :, u * UNIT : (u + 1) * UNIT], y[:])
             stage[u] = y
 
+        def fetch_ut(u):
+            side[u] = work.tile([P, PACK, UNIT], F32, name="ut_sb")
+            nc.scalar.copy(side[u][:], banks[UT, u][:])
+
+        def ut_minus_uxx(u):
+            part = work.tile([P, PACK, UNIT], F32, name="part")
+            nc.vector.scalar_tensor_tensor(
+                part[:].rearrange("p t j -> p (t j)"),
+                banks[UXX, u][:].rearrange("p t j -> p (t j)"),
+                -0.3,
+                side[u][:].rearrange("p t j -> p (t j)"),
+                MULT,
+                ADD,
+            )
+            side[u] = part
+
+        def add_up(u):
+            y = keep.tile([P, PACK, UNIT], F32, name=f"y{u}")
+            nc.gpsimd.tensor_tensor(y[:], stage[u][:], side[u][:], ADD)
+            nc.sync.dma_start(out_rows[:, :, u * UNIT : (u + 1) * UNIT], y[:])
+            stage[u] = y
+
         def round_y(u, engine_copy):
             y_bf = work.tile([P, PACK * UNIT], BF16, align_bytes=64, name="y_bf")
             interleave(engine_copy, y_bf[:], stage[u][:])
@@ -246,66 +302,69 @@ def tile_picked_ypinn_burg_po_kernel(
             nc.sync.dma_start(out_words[:, cols], y_codes[:, cols].bitcast(I32))
 
         vcopy, scopy = nc.vector.tensor_copy, nc.scalar.copy
-        hid = {}
-        hid[0] = hidden(0)
-        scaled(U0, 0, False)
-        scaled(UX, 0, True)
-        scaled(UT, 0, True)
-        hid[1] = hidden(1)
-        weave(U0, 0, vcopy)
-        weave(U0, 1, vcopy)
-        deal_weight(vcopy, w2_bf, w2_raw, 0, P)
-        weave(UX, 0, vcopy)
+        first_layer(0)
+        tanh(0)
+        square(0)
+        first_layer(1)
+        deal_weight(vcopy, w2_bf, w2_raw[0], 0, 64, 0)
+        deal_weight(vcopy, w2_bf, w2_raw[1], 64, 128, 64)
+        direct_u0(0)
+        scaled(UX, 0, 2, nc.scalar, "ux0")
+        scaled(HC, 0, 2, nc.scalar, "hc0")
+        tanh(1)
+        scaled(UT, 0, 2, nc.vector, "ut0")
         nc.vector.quantize_mx(w2_codes[:].bitcast(FP8X4), w2_scales[:], w2_bf[:])
-        second(0)
-        heads(0, 0)
-        fetch_u0(0)
-        scaled(UX, 1, True)
-        scaled(U0, 1, True)
-        weave(UT, 0, vcopy)
-        weave(UXX, 0, vcopy)
+        direct_u0(1)
+        heads((U0, 0), (U0, 1))
+        weave(UX, 0, vcopy)
         weave(UX, 1, vcopy)
-        heads(0, 1)
-        weave(UT, 1, vcopy)
-        heads(1, 0)
+        square(1)
+        fetch_u0(0)
         fetch_u0(1)
-        scaled(UT, 1, True)
-        weave(UXX, 1, vcopy)
+        heads((UX, 0), (UX, 1))
+        weave(UT, 0, vcopy)
+        weave(UT, 1, vcopy)
+        direct_uxx(0)
+        heads((UT, 0), (UT, 1))
+        direct_uxx(1)
+        heads((UXX, 0), (UXX, 1))
+        scaled(UX, 2, 2, nc.scalar, "ux1")
+        scaled(U0, 2, 2, nc.gpsimd, "ux0")
+        scaled(HC, 2, 2, nc.gpsimd, "hc0")
+        scaled(UT, 2, 2, nc.scalar, "ut1")
         times_ux(0)
-        heads(1, 1)
-        plus_ut(0)
-        second(1)
-        minus_uxx(0)
-        round_y(0, scopy)
-        weave(UX, 2, vcopy)
         times_ux(1)
-        weave(U0, 2, vcopy)
-        weave(UT, 2, scopy)
+        plus_ut(0)
         plus_ut(1)
-        heads(2, 0)
-        fetch_u0(2)
-        weave(U0, 3, scopy)
-        weave(UX, 3, scopy)
-        weave(UXX, 2, vcopy)
+        minus_uxx(0)
         minus_uxx(1)
-        heads(2, 1)
-        weave(UT, 3, scopy)
-        weave(UXX, 3, scopy)
-        pack_y(0)
-        times_ux(2)
-        heads(3, 0)
+        weave(U0, 2, scopy)
+        weave(U0, 3, scopy)
+        weave(UX, 2, scopy)
+        weave(UX, 3, scopy)
+        direct_uxx(2)
+        heads((U0, 2), (U0, 3))
+        direct_uxx(3)
+        weave(UT, 2, vcopy)
+        fetch_u0(2)
         fetch_u0(3)
+        heads((UX, 2), (UX, 3))
+        heads((UT, 2), (UXX, 2))
+        weave(UT, 3, scopy)
+        heads((UT, 3), (UXX, 3))
+        round_y(0, scopy)
         round_y(1, scopy)
-        plus_ut(2)
-        heads(3, 1)
-        minus_uxx(2)
-        round_y(2, scopy)
+        times_ux(2)
         times_ux(3)
-        pack_y(1)
+        plus_ut(2)
+        pack_y(0)
         plus_ut(3)
-        pack_y(2)
+        pack_y(1)
+        minus_uxx(2)
         minus_uxx(3)
+        round_y(2, scopy)
         round_y(3, vcopy)
+        pack_y(2)
         pack_y(3)
         for q in range(4):
             queue = nc.sync if q % 2 == 0 else nc.scalar

@@ -20,22 +20,23 @@ PACK = 4
 CHUNK = 256
 UNIT = 128
 M_SPLIT = 48
+WARM = 256
 U0, UX, UT, UXX, HC = 0, 1, 2, 3, 4
 
 
 def deal_weight(engine_copy, grouped, raw, m0, m1, first=0):
     engine_copy(
-        grouped[:].rearrange("p (t m r) -> p m r t", t=PACK, r=PACK)[:, m0:m1],
-        raw[:].rearrange("p r (m t) -> p m r t", t=PACK)[:, m0 - first : m1 - first],
+        grouped[:].rearrange("p (a e m r) -> p a m r e", a=2, e=2, r=PACK)[:, :, m0:m1],
+        raw[:].rearrange("p r (m a e) -> p a m r e", a=2, e=2)[:, :, m0 - first : m1 - first],
     )
 
 
 def woven(grouped):
-    return grouped.rearrange("p (c i t) -> p c t i", t=PACK, i=4)
+    return grouped.rearrange("p (c i t) -> p c t i", t=PACK, i=2)
 
 
 def slotted(slots):
-    return slots.rearrange("p t (c i) -> p c t i", i=4)
+    return slots.rearrange("p t (c i) -> p c t i", i=2)
 
 
 def interleave(engine_copy, grouped, slots):
@@ -60,19 +61,14 @@ def tile_picked_ypinn_burg_po_kernel(
             else:
                 engine.tensor_scalar(out, in_, scale, zero[:] if bias is None else bias, MULT, ADD)
 
-        unit_c = keep.tile([P, PACK], F32)
-        wx_c = keep.tile([P, PACK], F32)
-        wt_c = keep.tile([P, PACK], F32)
-        scale_table = keep.tile([P, T], U8, align_bytes=64)
+        scale_table = keep.tile([P, T], U8, align_bytes=64, tag="w1_codes")
         nc.vector.memset(scale_table[:].bitcast(I32), 0)
-        warm = keep.tile([P, 1], F32, tag="words", align_bytes=64)
-        warm_mid = keep.tile([P, 1], F32, tag="w2_0")
-        warm_out = keep.tile([P, 1], F32, tag="w2_1")
-        nc.vector.memset(warm[:], 0.0)
+        warm = keep.tile([P, WARM], F32, tag="words", align_bytes=64)
+        warm_tanh = keep.tile([P, WARM], F32, tag="factors")
+        warm_square = keep.tile([P, 1], F32, tag="w2_0")
+        warm_copy = keep.tile([P, 1], F32, tag="w2_1")
         zero = keep.tile([P, 1], F32)
-        nc.vector.tensor_copy(zero[:], warm[:])
-        for column, vec in ((unit_c, unit), (wx_c, wx), (wt_c, wt)):
-            nc.gpsimd.dma_start(column[:], vec.rearrange("(p t) o -> p (t o)", t=PACK))
+        nc.gpsimd.memset(warm[:], 0.0)
 
         w1_raw = keep.tile([P, PACK, H], F32)
         nc.sync.dma_start(w1_raw[:], w1.rearrange("(p r) c -> p r c", r=PACK))
@@ -83,12 +79,18 @@ def tile_picked_ypinn_burg_po_kernel(
                 scale_table[32 * q : 32 * q + 4, :].bitcast(I32),
                 x_scales[0, 4 * q : 4 * q + 4, :].bitcast(I32),
             )
-        nc.scalar.activation(warm_mid[:], zero[:], ACT.Tanh)
-        nc.scalar.activation(warm_out[:], warm_mid[:], ACT.Square)
+        nc.scalar.activation(warm_tanh[:], warm[:], ACT.Tanh)
+        nc.scalar.activation(warm_square[:], warm_tanh[:, 0:1], ACT.Square)
+        nc.scalar.copy(warm_copy[:], warm_square[:])
+        nc.scalar.copy(zero[:], warm_copy[:])
         word_table = keep.tile([P, T], U32, tag="words", align_bytes=64)
         nc.sync.dma_start(
             word_table[:].bitcast(I32), x_words[0].rearrange("p n t -> p (n t)").bitcast(I32)
         )
+        factors = keep.tile([P, 3, 8], F32, tag="factors")
+        unit_c, wx_c, wt_c = (factors[:, n, 0:PACK] for n in range(3))
+        for column, vec in ((unit_c, unit), (wx_c, wx), (wt_c, wt)):
+            nc.sync.dma_start(column, vec.rearrange("(p t) o -> p (t o)", t=PACK))
         w2_raw = []
         for half in range(2):
             raw = keep.tile([P, PACK, N // 2], F32, tag=f"w2_{half}", name=f"w2_raw{half}")
@@ -97,7 +99,7 @@ def tile_picked_ypinn_burg_po_kernel(
             w2_raw.append(raw)
 
         w1_bf = keep.tile([P, PACK * H], BF16, align_bytes=64)
-        w1_codes = keep.tile([P, H], U32, align_bytes=64)
+        w1_codes = keep.tile([P, H], U32, align_bytes=64, tag="w1_codes")
         w1_scales = keep.tile([P, H], U8, align_bytes=64)
         deal_weight(nc.vector.tensor_copy, w1_bf, w1_raw, 0, M_SPLIT)
         deal_weight(nc.scalar.copy, w1_bf, w1_raw, M_SPLIT, P)
@@ -115,10 +117,10 @@ def tile_picked_ypinn_burg_po_kernel(
         neg_ut = keep.tile([P, PACK], F32)
         neg_ux = keep.tile([P, PACK], F32)
         c_xx = keep.tile([P, PACK], F32)
-        nc.gpsimd.tensor_tensor(c_ux[:], unit_c[:], wx_c[:], MULT)
+        nc.gpsimd.tensor_tensor(c_ux[:], unit_c, wx_c, MULT)
         nc.gpsimd.tensor_scalar(neg_ux[:], c_ux[:], -1.0, 0.0, MULT, ADD)
-        nc.gpsimd.tensor_scalar(c_xx[:], wx_c[:], -2.0, 0.0, MULT, ADD)
-        nc.gpsimd.tensor_tensor(c_ut[:], unit_c[:], wt_c[:], MULT)
+        nc.gpsimd.tensor_scalar(c_xx[:], wx_c, -2.0, 0.0, MULT, ADD)
+        nc.gpsimd.tensor_tensor(c_ut[:], unit_c, wt_c, MULT)
         nc.gpsimd.tensor_scalar(neg_ut[:], c_ut[:], -1.0, 0.0, MULT, ADD)
 
         for c in range(S // CHUNK):
@@ -197,10 +199,10 @@ def tile_picked_ypinn_burg_po_kernel(
         def scaled(kind, first, count, engine, tag):
             c, lo = divmod(first * UNIT, CHUNK)
             src, scale, bias, dtype = {
-                U0: (hid, unit_c, None, BF16),
+                U0: (hid, unit_c, None, F32),
                 HC: (hid, c_xx, None, F32),
                 UX: (squares, neg_ux, c_ux, F32),
-                UT: (squares, neg_ut, c_ut, BF16),
+                UT: (squares, neg_ut, c_ut, F32),
             }[kind]
             slots = keep.tile([P, PACK, count * UNIT], dtype, name=f"z{kind}_{first}", tag=tag)
             for t in range(PACK):
@@ -219,7 +221,7 @@ def tile_picked_ypinn_burg_po_kernel(
             interleave(engine_copy, target(kind, u), z[kind, u])
 
         def direct_u0(u):
-            spread = unit_c[:].unsqueeze(1).unsqueeze(3).to_broadcast([P, UNIT // 4, PACK, 4])
+            spread = unit_c.unsqueeze(1).unsqueeze(3).to_broadcast([P, UNIT // 2, PACK, 2])
             nc.vector.tensor_tensor(woven(target(U0, u)), slotted(of_unit(hid, u)), spread, MULT)
 
         def direct_uxx(u):

@@ -172,6 +172,9 @@ def tile_picked_ypinn_burg_po_kernel(
         banks = {}
         stage = {}
         side = {}
+        both = {}
+        whole = {}
+        y_bf = {}
         def pair_up(*members):
             name = "_".join(f"{kind}{u}" for kind, u in members)
             wide = keep.tile([P, 2, PACK * UNIT], BF16, align_bytes=64, name=f"grouped{name}")
@@ -182,12 +185,13 @@ def tile_picked_ypinn_burg_po_kernel(
             )
             for e, member in enumerate(members):
                 grouped[member] = wide[:, e, :]
+            both[members[0]] = wide[:].rearrange("p k c -> p (k c)")
 
         pair_up((U0, 0), (U0, 1))
         pair_up((UX, 0), (UX, 1))
         pair_up((UT, 0), (UT, 1))
-        pair_up((UXX, 0), (UXX, 1))
         pair_up((U0, 2), (U0, 3))
+        pair_up((UXX, 0), (UXX, 1))
         pair_up((UX, 2), (UX, 3))
         pair_up((UT, 2), (UXX, 2))
         pair_up((UT, 3), (UXX, 3))
@@ -211,6 +215,7 @@ def tile_picked_ypinn_burg_po_kernel(
                     engine, slots[:, t, :], src[c][:, t, lo : lo + count * UNIT], scale[:, col],
                     None if bias is None else bias[:, col],
                 )
+            whole[kind, first] = slots
             for n in range(count):
                 z[kind, first + n] = slots[:, :, n * UNIT : (n + 1) * UNIT]
 
@@ -226,6 +231,16 @@ def tile_picked_ypinn_burg_po_kernel(
 
         def direct_uxx(u):
             nc.vector.tensor_tensor(woven(target(UXX, u)), slotted(z[HC, u]), slotted(z[UX, u]), MULT)
+
+        def weave2(kind, u, engine_copy):
+            interleave(engine_copy, both[kind, u], whole[kind, u][:])
+
+        def direct2_u0(u):
+            spread = unit_c.unsqueeze(1).unsqueeze(3).to_broadcast([P, CHUNK // 2, PACK, 2])
+            nc.vector.tensor_tensor(woven(both[U0, u]), slotted(hid[u // 2][:]), spread, MULT)
+
+        def direct2_uxx(u):
+            nc.vector.tensor_tensor(woven(both[UXX, u]), slotted(whole[HC, u][:]), slotted(whole[UX, u][:]), MULT)
 
         def heads(*members):
             wide, codes, scales = packed[members]
@@ -294,13 +309,16 @@ def tile_picked_ypinn_burg_po_kernel(
             stage[u] = y
 
         def round_y(u, engine_copy):
-            y_bf = work.tile([P, PACK * UNIT], BF16, align_bytes=64, name="y_bf")
-            interleave(engine_copy, y_bf[:], stage[u][:])
-            stage[u] = y_bf
+            c, n = divmod(u, 2)
+            if c not in y_bf:
+                y_bf[c] = keep.tile([P, 2, PACK * UNIT], BF16, align_bytes=64, name=f"y_bf{c}")
+            interleave(engine_copy, y_bf[c][:, n, :], stage[u][:])
 
-        def pack_y(u):
-            cols = slice(u * UNIT, (u + 1) * UNIT)
-            nc.vector.quantize_mx(y_codes[:, cols].bitcast(FP8X4), y_scales[:, cols], stage[u][:])
+        def pack_y(c):
+            cols = slice(c * CHUNK, (c + 1) * CHUNK)
+            nc.vector.quantize_mx(
+                y_codes[:, cols].bitcast(FP8X4), y_scales[:, cols], y_bf[c][:].rearrange("p n c -> p (n c)")
+            )
             nc.sync.dma_start(out_words[:, cols], y_codes[:, cols].bitcast(I32))
 
         vcopy, scopy = nc.vector.tensor_copy, nc.scalar.copy
@@ -310,64 +328,55 @@ def tile_picked_ypinn_burg_po_kernel(
         first_layer(1)
         deal_weight(vcopy, w2_bf, w2_raw[0], 0, 64, 0)
         deal_weight(vcopy, w2_bf, w2_raw[1], 64, 128, 64)
-        direct_u0(0)
+        direct2_u0(0)
         scaled(UX, 0, 2, nc.scalar, "ux0")
         scaled(HC, 0, 2, nc.scalar, "hc0")
         tanh(1)
-        scaled(UT, 0, 2, nc.vector, "ut0")
         nc.vector.quantize_mx(w2_codes[:].bitcast(FP8X4), w2_scales[:], w2_bf[:])
-        direct_u0(1)
+        scaled(UT, 0, 2, nc.vector, "ut0")
         heads((U0, 0), (U0, 1))
-        weave(UX, 0, vcopy)
-        weave(UX, 1, vcopy)
-        square(1)
+        weave2(UX, 0, vcopy)
         fetch_u0(0)
         fetch_u0(1)
+        square(1)
+        weave2(UT, 0, vcopy)
         heads((UX, 0), (UX, 1))
-        weave(UT, 0, vcopy)
-        weave(UT, 1, vcopy)
-        direct_uxx(0)
+        direct2_u0(2)
         heads((UT, 0), (UT, 1))
-        direct_uxx(1)
+        direct2_uxx(0)
+        heads((U0, 2), (U0, 3))
         heads((UXX, 0), (UXX, 1))
         scaled(UX, 2, 2, nc.scalar, "ux1")
-        scaled(U0, 2, 2, nc.gpsimd, "ux0")
         scaled(HC, 2, 2, nc.gpsimd, "hc0")
+        weave2(UX, 2, scopy)
         scaled(UT, 2, 2, nc.scalar, "ut1")
+        weave(UT, 2, scopy)
+        fetch_u0(2)
+        weave(UT, 3, scopy)
+        fetch_u0(3)
         times_ux(0)
         times_ux(1)
         plus_ut(0)
         plus_ut(1)
         minus_uxx(0)
         minus_uxx(1)
-        weave(U0, 2, scopy)
-        weave(U0, 3, scopy)
-        weave(UX, 2, scopy)
-        weave(UX, 3, scopy)
-        direct_uxx(2)
-        heads((U0, 2), (U0, 3))
-        direct_uxx(3)
-        weave(UT, 2, vcopy)
-        fetch_u0(2)
-        fetch_u0(3)
         heads((UX, 2), (UX, 3))
+        direct_uxx(2)
+        direct_uxx(3)
         heads((UT, 2), (UXX, 2))
-        weave(UT, 3, scopy)
-        heads((UT, 3), (UXX, 3))
         round_y(0, scopy)
         round_y(1, scopy)
         times_ux(2)
+        heads((UT, 3), (UXX, 3))
         times_ux(3)
         plus_ut(2)
         pack_y(0)
         plus_ut(3)
-        pack_y(1)
         minus_uxx(2)
         minus_uxx(3)
         round_y(2, scopy)
         round_y(3, vcopy)
-        pack_y(2)
-        pack_y(3)
+        pack_y(1)
         for q in range(4):
             queue = nc.sync if q % 2 == 0 else nc.scalar
             queue.dma_start(

@@ -2,7 +2,7 @@ from contextlib import ExitStack
 
 import concourse.mybir as mybir
 
-K, T, S, H, N = 512, 2048, 512, 512, 512
+T, S, H, N = 2048, 512, 512, 512
 FLOPS = 5 * 2 * 512 * 512 * 512
 
 F32 = mybir.dt.float32
@@ -17,72 +17,72 @@ MULT, ADD = mybir.AluOpType.mult, mybir.AluOpType.add
 
 P = 128
 PACK = 4
+QUADRANTS = 4
 CHUNK = 256
 UNIT = 128
-M_SPLIT = 48
-WARM = 256
-U0, UX, UT, UXX, HC = 0, 1, 2, 3, 4
+W1_ON_VECTOR = 48
+WARM = 192
+U0, UX, UT, UXX = "u0", "ux", "ut", "uxx"
+HX = "hx"
 
 
-def deal_weight(engine_copy, grouped, raw, m0, m1, first=0):
-    engine_copy(
-        grouped[:].rearrange("p (a e m r) -> p a m r e", a=2, e=2, r=PACK)[:, :, m0:m1],
-        raw[:].rearrange("p r (m a e) -> p a m r e", a=2, e=2)[:, :, m0 - first : m1 - first],
-    )
+def deal_weight(engine_copy, woven_weight, raw, first, groups):
+    dealt = woven_weight.rearrange("p (a e m r) -> p a m r e", a=2, e=2, r=PACK)
+    engine_copy(dealt[:, :, first : first + groups], raw)
 
 
-def woven(grouped):
-    return grouped.rearrange("p (c i t) -> p c t i", t=PACK, i=2)
+def weight_walk(raw):
+    return raw.rearrange("p r (m a e) -> p a m r e", a=2, e=2)
 
 
-def slotted(slots):
-    return slots.rearrange("p t (c i) -> p c t i", i=2)
+def woven_walk(woven):
+    return woven.rearrange("p (c i t) -> p c t i", t=PACK, i=2)
 
 
-def interleave(engine_copy, grouped, slots):
-    engine_copy(woven(grouped), slotted(slots))
+def slotted_walk(slotted):
+    return slotted.rearrange("p t (c i) -> p c t i", i=2)
+
+
+def flat(slotted):
+    return slotted.rearrange("p t j -> p (t j)")
 
 
 def tile_picked_ypinn_burg_po_kernel(
     tc, x_words, x_scales, w1, unit, wx, wt, w2, offs, out_0, out_1, out_2
 ):
     nc = tc.nc
+    chunks = range(S // CHUNK)
     with ExitStack() as ctx:
         keep = ctx.enter_context(tc.tile_pool(name="keep", bufs=1))
         work = ctx.enter_context(tc.tile_pool(name="work", bufs=2))
         psum = ctx.enter_context(tc.psum_pool(name="psum", bufs=8))
 
-        def affine(engine, out, in_, scale, bias):
-            if engine is nc.scalar:
-                if bias is None:
-                    nc.scalar.activation(out, in_, ACT.Copy, scale=scale)
-                else:
-                    nc.scalar.activation(out, in_, ACT.Identity, bias=bias, scale=scale)
-            else:
-                engine.tensor_scalar(out, in_, scale, zero[:] if bias is None else bias, MULT, ADD)
-
         scale_table = keep.tile([P, T], U8, align_bytes=64, tag="w1_codes")
         nc.vector.memset(scale_table[:].bitcast(I32), 0)
+
         warm = keep.tile([P, WARM], F32, tag="words", align_bytes=64)
         warm_tanh = keep.tile([P, WARM], F32, tag="factors")
         warm_square = keep.tile([P, 1], F32, tag="w2_0")
         warm_copy = keep.tile([P, 1], F32, tag="w2_1")
         zero = keep.tile([P, 1], F32)
+        seed = keep.tile([P, WARM], F32)
         nc.gpsimd.memset(warm[:], 0.0)
+        nc.gpsimd.tensor_copy(seed[:], warm[:])
 
         w1_raw = keep.tile([P, PACK, H], F32)
         nc.sync.dma_start(w1_raw[:], w1.rearrange("(p r) c -> p r c", r=PACK))
         offsets = keep.tile([P, S // 16], U16)
         nc.sync.dma_start(offsets[:], offs)
-        for q in range(4):
+        for q in range(QUADRANTS):
             nc.sync.dma_start(
                 scale_table[32 * q : 32 * q + 4, :].bitcast(I32),
                 x_scales[0, 4 * q : 4 * q + 4, :].bitcast(I32),
             )
-        nc.scalar.activation(warm_tanh[:], warm[:], ACT.Tanh)
+        nc.scalar.activation(warm_tanh[:], seed[:], ACT.Tanh)
         nc.scalar.activation(warm_square[:], warm_tanh[:, 0:1], ACT.Square)
         nc.scalar.copy(warm_copy[:], warm_square[:])
         nc.scalar.copy(zero[:], warm_copy[:])
+
         word_table = keep.tile([P, T], U32, tag="words", align_bytes=64)
         nc.sync.dma_start(
             word_table[:].bitcast(I32), x_words[0].rearrange("p n t -> p (n t)").bitcast(I32)
@@ -98,286 +98,222 @@ def tile_picked_ypinn_burg_po_kernel(
             nc.sync.dma_start(raw[:], w2.rearrange("(p r) c -> p r c", r=PACK)[:, :, cols])
             w2_raw.append(raw)
 
-        w1_bf = keep.tile([P, PACK * H], BF16, align_bytes=64)
+        w1_woven = keep.tile([P, PACK * H], BF16, align_bytes=64)
         w1_codes = keep.tile([P, H], U32, align_bytes=64, tag="w1_codes")
         w1_scales = keep.tile([P, H], U8, align_bytes=64)
-        deal_weight(nc.vector.tensor_copy, w1_bf, w1_raw, 0, M_SPLIT)
-        deal_weight(nc.scalar.copy, w1_bf, w1_raw, M_SPLIT, P)
+        w1_walk = weight_walk(w1_raw[:])
+        deal_weight(nc.vector.tensor_copy, w1_woven[:], w1_walk[:, :, :W1_ON_VECTOR], 0, W1_ON_VECTOR)
+        deal_weight(nc.scalar.copy, w1_woven[:], w1_walk[:, :, W1_ON_VECTOR:], W1_ON_VECTOR, P - W1_ON_VECTOR)
 
-        x_codes, x_bytes = [], []
-        for c in range(S // CHUNK):
-            picked = keep.tile([P, CHUNK], U8, align_bytes=64, name=f"x_bytes{c}")
-            lst = offsets[:, c * CHUNK // 16 : (c + 1) * CHUNK // 16]
-            nc.vector.tensor_copy(picked[:], scale_table[:].indirect(lst))
-            x_bytes.append(picked)
-        nc.vector.quantize_mx(w1_codes[:].bitcast(FP8X4), w1_scales[:], w1_bf[:])
+        def gather(table, dtype, name):
+            picked = []
+            for c in chunks:
+                columns = keep.tile([P, CHUNK], dtype, align_bytes=64, name=f"{name}{c}")
+                entries = offsets[:, c * CHUNK // 16 : (c + 1) * CHUNK // 16]
+                nc.vector.tensor_copy(columns[:], table[:].indirect(entries))
+                picked.append(columns)
+            return picked
 
-        c_ut = keep.tile([P, PACK], F32)
-        c_ux = keep.tile([P, PACK], F32)
-        neg_ut = keep.tile([P, PACK], F32)
-        neg_ux = keep.tile([P, PACK], F32)
-        c_xx = keep.tile([P, PACK], F32)
-        nc.gpsimd.tensor_tensor(c_ux[:], unit_c, wx_c, MULT)
-        nc.gpsimd.tensor_scalar(neg_ux[:], c_ux[:], -1.0, 0.0, MULT, ADD)
-        nc.gpsimd.tensor_scalar(c_xx[:], wx_c, -2.0, 0.0, MULT, ADD)
-        nc.gpsimd.tensor_tensor(c_ut[:], unit_c, wt_c, MULT)
-        nc.gpsimd.tensor_scalar(neg_ut[:], c_ut[:], -1.0, 0.0, MULT, ADD)
+        x_bytes = gather(scale_table, U8, "x_bytes")
+        nc.vector.quantize_mx(w1_codes[:].bitcast(FP8X4), w1_scales[:], w1_woven[:])
 
-        for c in range(S // CHUNK):
-            picked = keep.tile([P, CHUNK], U32, align_bytes=64, name=f"x_codes{c}")
-            lst = offsets[:, c * CHUNK // 16 : (c + 1) * CHUNK // 16]
-            nc.vector.tensor_copy(picked[:], word_table[:].indirect(lst))
-            x_codes.append(picked)
+        gains = keep.tile([P, 2, PACK], F32)
+        neg_gains = keep.tile([P, 2, PACK], F32)
+        minus_2wx = keep.tile([P, PACK], F32)
+        nc.vector.tensor_tensor(
+            gains[:], factors[:, 1:3, 0:PACK], unit_c.unsqueeze(1).to_broadcast([P, 2, PACK]), MULT
+        )
+        nc.scalar.mul(neg_gains[:], gains[:], -1.0)
+        nc.scalar.mul(minus_2wx[:], wx_c, -2.0)
 
-        pre, hid, squares = {}, {}, {}
-
-        def first_layer(c):
-            for pair in range(2):
-                bank = psum.tile([P, 2, CHUNK], F32, name="bank")
-                for e in range(2):
-                    t = 2 * pair + e
-                    nc.tensor.matmul_mx(
-                        bank[:, e, :],
-                        lhsT=w1_codes[:, t * P : (t + 1) * P].bitcast(FP8X4),
-                        lhsT_scale=w1_scales[:, t * P : (t + 1) * P],
-                        rhs=x_codes[c][:].bitcast(FP8X4),
-                        rhs_scale=x_bytes[c][:],
-                        start=True,
-                        stop=True,
-                    )
-                pre[c, pair] = bank
-
-        def tanh(c):
-            hid[c] = keep.tile([P, PACK, CHUNK], F32, name=f"h{c}")
-            for pair in range(2):
-                nc.scalar.activation(hid[c][:, 2 * pair : 2 * pair + 2, :], pre[c, pair][:], ACT.Tanh)
-
-        def square(c):
-            squares[c] = keep.tile([P, PACK, CHUNK], F32, name=f"sq{c}")
-            for pair in range(2):
-                ts = slice(2 * pair, 2 * pair + 2)
-                nc.scalar.activation(squares[c][:, ts, :], hid[c][:, ts, :], ACT.Square)
+        x_codes = gather(word_table, U32, "x_codes")
 
         y_codes = keep.tile([P, S], U32, align_bytes=64)
         y_scales = keep.tile([P, S], U8, align_bytes=64)
         out_rows = out_0.rearrange("(p t) j -> p t j", t=PACK)
         out_words = out_1[0].rearrange("p n t -> p (n t)").bitcast(I32)
-        w2_bf = keep.tile([P, PACK * N], BF16, align_bytes=64)
+        w2_woven = keep.tile([P, PACK * N], BF16, align_bytes=64)
         w2_codes = keep.tile([P, N], U32, align_bytes=64)
         w2_scales = keep.tile([P, N], U8, align_bytes=64)
 
-        z = {}
-        grouped = {}
-        packed = {}
-        banks = {}
-        stage = {}
-        side = {}
-        both = {}
-        whole = {}
-        y_bf = {}
-        def pair_up(*members):
-            name = "_".join(f"{kind}{u}" for kind, u in members)
-            wide = keep.tile([P, 2, PACK * UNIT], BF16, align_bytes=64, name=f"grouped{name}")
-            packed[members] = (
-                wide,
-                keep.tile([P, 2 * UNIT], U32, align_bytes=64, name=f"codes{name}"),
-                keep.tile([P, 2 * UNIT], U8, align_bytes=64, name=f"scales{name}"),
-            )
-            for e, member in enumerate(members):
-                grouped[member] = wide[:, e, :]
-            both[members[0]] = wide[:].rearrange("p k c -> p (k c)")
-
-        pair_up((U0, 0), (U0, 1))
-        pair_up((UX, 0), (UX, 1))
-        pair_up((UT, 0), (UT, 1))
-        pair_up((U0, 2), (U0, 3))
-        pair_up((UXX, 0), (UXX, 1))
-        pair_up((UX, 2), (UX, 3))
-        pair_up((UT, 2), (UXX, 2))
-        pair_up((UT, 3), (UXX, 3))
-
-        def of_unit(tiles, u):
-            c, lo = divmod(u * UNIT, CHUNK)
-            return tiles[c][:, :, lo : lo + UNIT]
-
-        def scaled(kind, first, count, engine, tag):
-            c, lo = divmod(first * UNIT, CHUNK)
-            src, scale, bias, dtype = {
-                U0: (hid, unit_c, None, F32),
-                HC: (hid, c_xx, None, F32),
-                UX: (squares, neg_ux, c_ux, F32),
-                UT: (squares, neg_ut, c_ut, F32),
-            }[kind]
-            slots = keep.tile([P, PACK, count * UNIT], dtype, name=f"z{kind}_{first}", tag=tag)
-            for t in range(PACK):
-                col = slice(t, t + 1)
-                affine(
-                    engine, slots[:, t, :], src[c][:, t, lo : lo + count * UNIT], scale[:, col],
-                    None if bias is None else bias[:, col],
+        z_woven, z_codes, z_scales = {}, {}, {}
+        for c in chunks:
+            for kind in (U0, UX, UXX, UT):
+                name = f"{kind}{c}"
+                z_woven[kind, c] = keep.tile(
+                    [P, PACK * CHUNK], BF16, align_bytes=64, name=f"woven_{name}", tag=f"woven_{name}"
                 )
-            whole[kind, first] = slots
-            for n in range(count):
-                z[kind, first + n] = slots[:, :, n * UNIT : (n + 1) * UNIT]
+                z_codes[kind, c] = keep.tile([P, CHUNK], U32, align_bytes=64, name=f"codes_{name}")
+                z_scales[kind, c] = keep.tile([P, CHUNK], U8, align_bytes=64, name=f"scales_{name}")
 
-        def target(kind, u):
-            return grouped[kind, u]
+        pre, h, h_squared, slotted, banks, running, y_woven = {}, {}, {}, {}, {}, {}, {}
 
-        def weave(kind, u, engine_copy):
-            interleave(engine_copy, target(kind, u), z[kind, u])
+        def product(out, codes, scales, t, moving_codes, moving_scales):
+            nc.tensor.matmul_mx(
+                out,
+                lhsT=codes[:, t * P : (t + 1) * P].bitcast(FP8X4),
+                lhsT_scale=scales[:, t * P : (t + 1) * P],
+                rhs=moving_codes.bitcast(FP8X4),
+                rhs_scale=moving_scales,
+                start=True,
+                stop=True,
+            )
 
-        def direct_u0(u):
-            spread = unit_c.unsqueeze(1).unsqueeze(3).to_broadcast([P, UNIT // 2, PACK, 2])
-            nc.vector.tensor_tensor(woven(target(U0, u)), slotted(of_unit(hid, u)), spread, MULT)
+        def first_layer(c):
+            for pair in range(2):
+                pre[c, pair] = psum.tile([P, 2, CHUNK], F32, name="bank")
+                for e in range(2):
+                    product(pre[c, pair][:, e, :], w1_codes, w1_scales, 2 * pair + e, x_codes[c][:], x_bytes[c][:])
 
-        def direct_uxx(u):
-            nc.vector.tensor_tensor(woven(target(UXX, u)), slotted(z[HC, u]), slotted(z[UX, u]), MULT)
+        def tanh(c):
+            h[c] = keep.tile([P, PACK, CHUNK], F32, name=f"h{c}")
+            for pair in range(2):
+                nc.scalar.activation(h[c][:, 2 * pair : 2 * pair + 2, :], pre[c, pair][:], ACT.Tanh)
 
-        def weave2(kind, u, engine_copy):
-            interleave(engine_copy, both[kind, u], whole[kind, u][:])
+        def square(c):
+            h_squared[c] = keep.tile([P, PACK, CHUNK], F32, name=f"h_squared{c}")
+            for pair in range(2):
+                slots = slice(2 * pair, 2 * pair + 2)
+                nc.scalar.activation(h_squared[c][:, slots, :], h[c][:, slots, :], ACT.Square)
 
-        def direct2_u0(u):
+        def new_slotted(kind, c, tag):
+            slotted[kind, c] = keep.tile([P, PACK, CHUNK], F32, name=f"{kind}{c}", tag=tag, align_bytes=64)
+            return slotted[kind, c]
+
+        def slope(kind, c):
+            row = (UX, UT).index(kind)
+            z = new_slotted(kind, c, f"{kind}{c}")
+            for t in range(PACK):
+                nc.scalar.activation(
+                    z[:, t, :], h_squared[c][:, t, :], ACT.Identity,
+                    bias=gains[:, row, t : t + 1], scale=neg_gains[:, row, t : t + 1],
+                )
+
+        def hx_on_scalar(c):
+            hx = new_slotted(HX, c, f"{HX}{c}")
+            for t in range(PACK):
+                nc.scalar.activation(hx[:, t, :], h[c][:, t, :], ACT.Copy, scale=minus_2wx[:, t : t + 1])
+
+        def hx_on_gpsimd(c, tag):
+            hx = new_slotted(HX, c, tag)
+            for t in range(PACK):
+                nc.gpsimd.tensor_scalar(hx[:, t, :], h[c][:, t, :], minus_2wx[:, t : t + 1], zero[:], MULT, ADD)
+
+        def weave(kind, c, engine_copy):
+            engine_copy(woven_walk(z_woven[kind, c][:]), slotted_walk(slotted[kind, c][:]))
+
+        def woven_u0(c):
             spread = unit_c.unsqueeze(1).unsqueeze(3).to_broadcast([P, CHUNK // 2, PACK, 2])
-            nc.vector.tensor_tensor(woven(both[U0, u]), slotted(hid[u // 2][:]), spread, MULT)
+            nc.vector.tensor_tensor(woven_walk(z_woven[U0, c][:]), slotted_walk(h[c][:]), spread, MULT)
 
-        def direct2_uxx(u):
-            nc.vector.tensor_tensor(woven(both[UXX, u]), slotted(whole[HC, u][:]), slotted(whole[UX, u][:]), MULT)
+        def woven_uxx(c):
+            nc.vector.tensor_tensor(
+                woven_walk(z_woven[UXX, c][:]),
+                slotted_walk(slotted[HX, c][:]),
+                slotted_walk(slotted[UX, c][:]),
+                MULT,
+            )
 
-        def heads(*members):
-            wide, codes, scales = packed[members]
-            nc.vector.quantize_mx(codes[:].bitcast(FP8X4), scales[:], wide[:].rearrange("p k c -> p (k c)"))
-            for e, member in enumerate(members):
+        def heads(kind, c):
+            codes, scales = z_codes[kind, c], z_scales[kind, c]
+            nc.vector.quantize_mx(codes[:].bitcast(FP8X4), scales[:], z_woven[kind, c][:])
+            for n in range(2):
                 bank = psum.tile([P, PACK, UNIT], F32, name="bank")
+                cols = slice(n * UNIT, (n + 1) * UNIT)
                 for t in range(PACK):
-                    nc.tensor.matmul_mx(
-                        bank[:, t, :],
-                        lhsT=w2_codes[:, t * P : (t + 1) * P].bitcast(FP8X4),
-                        lhsT_scale=w2_scales[:, t * P : (t + 1) * P],
-                        rhs=codes[:, e * UNIT : (e + 1) * UNIT].bitcast(FP8X4),
-                        rhs_scale=scales[:, e * UNIT : (e + 1) * UNIT],
-                        start=True,
-                        stop=True,
-                    )
-                banks[member] = bank
+                    product(bank[:, t, :], w2_codes, w2_scales, t, codes[:, cols], scales[:, cols])
+                banks[kind, 2 * c + n] = bank
 
-        def fetch_u0(u):
-            stage[u] = work.tile([P, PACK, UNIT], F32, name="u0_sb")
-            nc.scalar.copy(stage[u][:], banks[U0, u][:])
+        def units(c):
+            return (2 * c, 2 * c + 1)
 
-        def times_ux(u):
-            prod = work.tile([P, PACK, UNIT], F32, name="prod")
-            nc.vector.tensor_tensor(prod[:], banks[UX, u][:], stage[u][:], MULT)
-            stage[u] = prod
+        def fetch_u0(c):
+            for u in units(c):
+                running[u] = work.tile([P, PACK, UNIT], F32, name="u0_sb")
+                nc.scalar.copy(running[u][:], banks[U0, u][:])
 
-        def plus_ut(u):
-            part = work.tile([P, PACK, UNIT], F32, name="part")
-            nc.vector.tensor_tensor(part[:], banks[UT, u][:], stage[u][:], ADD)
-            stage[u] = part
+        def times_ux(c):
+            for u in units(c):
+                prod = work.tile([P, PACK, UNIT], F32, name="prod")
+                nc.vector.tensor_tensor(prod[:], banks[UX, u][:], running[u][:], MULT)
+                running[u] = prod
 
-        def minus_uxx(u):
-            y = keep.tile([P, PACK, UNIT], F32, name=f"y{u}")
-            nc.vector.scalar_tensor_tensor(
-                y[:].rearrange("p t j -> p (t j)"),
-                banks[UXX, u][:].rearrange("p t j -> p (t j)"),
-                -0.3,
-                stage[u][:].rearrange("p t j -> p (t j)"),
-                MULT,
-                ADD,
-            )
-            nc.sync.dma_start(out_rows[:, :, u * UNIT : (u + 1) * UNIT], y[:])
-            stage[u] = y
+        def minus_uxx(c):
+            for u in units(c):
+                part = work.tile([P, PACK, UNIT], F32, name="part")
+                nc.vector.scalar_tensor_tensor(
+                    flat(part[:]), flat(banks[UXX, u][:]), -0.3, flat(running[u][:]), MULT, ADD
+                )
+                running[u] = part
 
-        def fetch_ut(u):
-            side[u] = work.tile([P, PACK, UNIT], F32, name="ut_sb")
-            nc.scalar.copy(side[u][:], banks[UT, u][:])
+        def plus_ut(c):
+            for u in units(c):
+                y = keep.tile([P, PACK, UNIT], F32, name=f"y{u}")
+                nc.vector.tensor_tensor(y[:], banks[UT, u][:], running[u][:], ADD)
+                nc.sync.dma_start(out_rows[:, :, u * UNIT : (u + 1) * UNIT], y[:])
+                running[u] = y
 
-        def ut_minus_uxx(u):
-            part = work.tile([P, PACK, UNIT], F32, name="part")
-            nc.vector.scalar_tensor_tensor(
-                part[:].rearrange("p t j -> p (t j)"),
-                banks[UXX, u][:].rearrange("p t j -> p (t j)"),
-                -0.3,
-                side[u][:].rearrange("p t j -> p (t j)"),
-                MULT,
-                ADD,
-            )
-            side[u] = part
-
-        def add_up(u):
-            y = keep.tile([P, PACK, UNIT], F32, name=f"y{u}")
-            nc.gpsimd.tensor_tensor(y[:], stage[u][:], side[u][:], ADD)
-            nc.sync.dma_start(out_rows[:, :, u * UNIT : (u + 1) * UNIT], y[:])
-            stage[u] = y
-
-        def round_y(u, engine_copy):
-            c, n = divmod(u, 2)
-            if c not in y_bf:
-                y_bf[c] = keep.tile([P, 2, PACK * UNIT], BF16, align_bytes=64, name=f"y_bf{c}")
-            interleave(engine_copy, y_bf[c][:, n, :], stage[u][:])
+        def round_y(c, engine_copies):
+            y_woven[c] = keep.tile([P, 2, PACK * UNIT], BF16, align_bytes=64, name=f"y_woven{c}")
+            for n, u in enumerate(units(c)):
+                engine_copies[n](woven_walk(y_woven[c][:, n, :]), slotted_walk(running[u][:]))
 
         def pack_y(c):
             cols = slice(c * CHUNK, (c + 1) * CHUNK)
             nc.vector.quantize_mx(
-                y_codes[:, cols].bitcast(FP8X4), y_scales[:, cols], y_bf[c][:].rearrange("p n c -> p (n c)")
+                y_codes[:, cols].bitcast(FP8X4), y_scales[:, cols], y_woven[c][:].rearrange("p n c -> p (n c)")
             )
             nc.sync.dma_start(out_words[:, cols], y_codes[:, cols].bitcast(I32))
 
-        vcopy, scopy = nc.vector.tensor_copy, nc.scalar.copy
+        on_vector, on_scalar = nc.vector.tensor_copy, nc.scalar.copy
+
         first_layer(0)
         tanh(0)
         square(0)
         first_layer(1)
-        deal_weight(vcopy, w2_bf, w2_raw[0], 0, 64, 0)
-        deal_weight(vcopy, w2_bf, w2_raw[1], 64, 128, 64)
-        direct2_u0(0)
-        scaled(UX, 0, 2, nc.scalar, "ux0")
-        scaled(HC, 0, 2, nc.scalar, "hc0")
+        for half in range(2):
+            deal_weight(on_vector, w2_woven[:], weight_walk(w2_raw[half][:]), half * P // 2, P // 2)
+        woven_u0(0)
+        slope(UX, 0)
+        hx_on_scalar(0)
         tanh(1)
-        nc.vector.quantize_mx(w2_codes[:].bitcast(FP8X4), w2_scales[:], w2_bf[:])
-        scaled(UT, 0, 2, nc.vector, "ut0")
-        heads((U0, 0), (U0, 1))
-        weave2(UX, 0, vcopy)
+        slope(UT, 0)
+        nc.vector.quantize_mx(w2_codes[:].bitcast(FP8X4), w2_scales[:], w2_woven[:])
+        heads(U0, 0)
+        weave(UX, 0, on_vector)
         fetch_u0(0)
-        fetch_u0(1)
         square(1)
-        weave2(UT, 0, vcopy)
-        heads((UX, 0), (UX, 1))
-        direct2_u0(2)
-        heads((UT, 0), (UT, 1))
-        direct2_uxx(0)
-        heads((U0, 2), (U0, 3))
-        heads((UXX, 0), (UXX, 1))
-        scaled(UX, 2, 2, nc.scalar, "ux1")
-        scaled(HC, 2, 2, nc.gpsimd, "hc0")
-        weave2(UX, 2, scopy)
-        scaled(UT, 2, 2, nc.scalar, "ut1")
-        weave(UT, 2, scopy)
-        fetch_u0(2)
-        weave(UT, 3, scopy)
-        fetch_u0(3)
+        heads(UX, 0)
+        woven_uxx(0)
+        woven_u0(1)
+        heads(UXX, 0)
+        weave(UT, 0, on_vector)
+        heads(U0, 1)
+        heads(UT, 0)
+
+        slope(UX, 1)
+        hx_on_gpsimd(1, f"woven_{UT}0")
+        weave(UX, 1, on_scalar)
+        fetch_u0(1)
+        slope(UT, 1)
+        weave(UT, 1, on_scalar)
         times_ux(0)
-        times_ux(1)
-        plus_ut(0)
-        plus_ut(1)
         minus_uxx(0)
+        plus_ut(0)
+
+        heads(UX, 1)
+        woven_uxx(1)
+        heads(UXX, 1)
+        times_ux(1)
+        heads(UT, 1)
+        round_y(0, (on_scalar, on_scalar))
         minus_uxx(1)
-        heads((UX, 2), (UX, 3))
-        direct_uxx(2)
-        direct_uxx(3)
-        heads((UT, 2), (UXX, 2))
-        round_y(0, scopy)
-        round_y(1, scopy)
-        times_ux(2)
-        heads((UT, 3), (UXX, 3))
-        times_ux(3)
-        plus_ut(2)
         pack_y(0)
-        plus_ut(3)
-        minus_uxx(2)
-        minus_uxx(3)
-        round_y(2, scopy)
-        round_y(3, vcopy)
+        plus_ut(1)
+        round_y(1, (on_scalar, on_vector))
         pack_y(1)
-        for q in range(4):
+
+        for q in range(QUADRANTS):
             queue = nc.sync if q % 2 == 0 else nc.scalar
             queue.dma_start(
                 out_2[0, 4 * q : 4 * q + 4, :].bitcast(I32),

from contextlib import ExitStack

import concourse.mybir as mybir

T, S, H, N = 2048, 512, 512, 512
FLOPS = 5 * 2 * 512 * 512 * 512

F32 = mybir.dt.float32
BF16 = mybir.dt.bfloat16
I32 = mybir.dt.int32
U32 = mybir.dt.uint32
U16 = mybir.dt.uint16
U8 = mybir.dt.uint8
FP8X4 = mybir.dt.float8_e4m3fn_x4
ACT = mybir.ActivationFunctionType
MULT, ADD = mybir.AluOpType.mult, mybir.AluOpType.add

P = 128
PACK = 4
QUADRANTS = 4
CHUNK = 256
UNIT = 128
W1_ON_VECTOR = 48
WARM = 192
U0, UX, UT, UXX = "u0", "ux", "ut", "uxx"
HX = "hx"


def deal_weight(engine_copy, woven_weight, raw, first, groups):
    dealt = woven_weight.rearrange("p (a e m r) -> p a m r e", a=2, e=2, r=PACK)
    engine_copy(dealt[:, :, first : first + groups], raw)


def weight_walk(raw):
    return raw.rearrange("p r (m a e) -> p a m r e", a=2, e=2)


def woven_walk(woven):
    return woven.rearrange("p (c i t) -> p c t i", t=PACK, i=2)


def slotted_walk(slotted):
    return slotted.rearrange("p t (c i) -> p c t i", i=2)


def flat(slotted):
    return slotted.rearrange("p t j -> p (t j)")


def tile_picked_ypinn_burg_po_kernel(
    tc, x_words, x_scales, w1, unit, wx, wt, w2, offs, out_0, out_1, out_2
):
    nc = tc.nc
    chunks = range(S // CHUNK)
    with ExitStack() as ctx:
        keep = ctx.enter_context(tc.tile_pool(name="keep", bufs=1))
        work = ctx.enter_context(tc.tile_pool(name="work", bufs=2))
        psum = ctx.enter_context(tc.psum_pool(name="psum", bufs=8))

        scale_table = keep.tile([P, T], U8, align_bytes=64, tag="w1_codes")
        nc.vector.memset(scale_table[:].bitcast(I32), 0)

        warm = keep.tile([P, WARM], F32, tag="words", align_bytes=64)
        warm_tanh = keep.tile([P, WARM], F32, tag="factors")
        warm_square = keep.tile([P, 1], F32, tag="w2_0")
        warm_copy = keep.tile([P, 1], F32, tag="w2_1")
        zero = keep.tile([P, 1], F32)
        seed = keep.tile([P, WARM], F32)
        nc.gpsimd.memset(warm[:], 0.0)
        nc.gpsimd.tensor_copy(seed[:], warm[:])

        w1_raw = keep.tile([P, PACK, H], F32)
        nc.sync.dma_start(w1_raw[:], w1.rearrange("(p r) c -> p r c", r=PACK))
        offsets = keep.tile([P, S // 16], U16)
        nc.sync.dma_start(offsets[:], offs)
        for q in range(QUADRANTS):
            nc.sync.dma_start(
                scale_table[32 * q : 32 * q + 4, :].bitcast(I32),
                x_scales[0, 4 * q : 4 * q + 4, :].bitcast(I32),
            )
        nc.scalar.activation(warm_tanh[:], seed[:], ACT.Tanh)
        nc.scalar.activation(warm_square[:], warm_tanh[:, 0:1], ACT.Square)
        nc.scalar.copy(warm_copy[:], warm_square[:])
        nc.scalar.copy(zero[:], warm_copy[:])

        word_table = keep.tile([P, T], U32, tag="words", align_bytes=64)
        nc.sync.dma_start(
            word_table[:].bitcast(I32), x_words[0].rearrange("p n t -> p (n t)").bitcast(I32)
        )
        factors = keep.tile([P, 3, 8], F32, tag="factors")
        unit_c, wx_c, wt_c = (factors[:, n, 0:PACK] for n in range(3))
        for column, vec in ((unit_c, unit), (wx_c, wx), (wt_c, wt)):
            nc.sync.dma_start(column, vec.rearrange("(p t) o -> p (t o)", t=PACK))
        w2_raw = []
        for half in range(2):
            raw = keep.tile([P, PACK, N // 2], F32, tag=f"w2_{half}", name=f"w2_raw{half}")
            cols = slice(half * N // 2, (half + 1) * N // 2)
            nc.sync.dma_start(raw[:], w2.rearrange("(p r) c -> p r c", r=PACK)[:, :, cols])
            w2_raw.append(raw)

        w1_woven = keep.tile([P, PACK * H], BF16, align_bytes=64)
        w1_codes = keep.tile([P, H], U32, align_bytes=64, tag="w1_codes")
        w1_scales = keep.tile([P, H], U8, align_bytes=64)
        w1_walk = weight_walk(w1_raw[:])
        deal_weight(nc.vector.tensor_copy, w1_woven[:], w1_walk[:, :, :W1_ON_VECTOR], 0, W1_ON_VECTOR)
        deal_weight(nc.scalar.copy, w1_woven[:], w1_walk[:, :, W1_ON_VECTOR:], W1_ON_VECTOR, P - W1_ON_VECTOR)

        def gather(table, dtype, name):
            picked = []
            for c in chunks:
                columns = keep.tile([P, CHUNK], dtype, align_bytes=64, name=f"{name}{c}")
                entries = offsets[:, c * CHUNK // 16 : (c + 1) * CHUNK // 16]
                nc.vector.tensor_copy(columns[:], table[:].indirect(entries))
                picked.append(columns)
            return picked

        x_bytes = gather(scale_table, U8, "x_bytes")
        nc.vector.quantize_mx(w1_codes[:].bitcast(FP8X4), w1_scales[:], w1_woven[:])

        gains = keep.tile([P, 2, PACK], F32)
        neg_gains = keep.tile([P, 2, PACK], F32)
        minus_2wx = keep.tile([P, PACK], F32)
        nc.vector.tensor_tensor(
            gains[:], factors[:, 1:3, 0:PACK], unit_c.unsqueeze(1).to_broadcast([P, 2, PACK]), MULT
        )
        nc.scalar.mul(neg_gains[:], gains[:], -1.0)
        nc.scalar.mul(minus_2wx[:], wx_c, -2.0)

        x_codes = gather(word_table, U32, "x_codes")

        y_codes = keep.tile([P, S], U32, align_bytes=64)
        y_scales = keep.tile([P, S], U8, align_bytes=64)
        out_rows = out_0.rearrange("(p t) j -> p t j", t=PACK)
        out_words = out_1[0].rearrange("p n t -> p (n t)").bitcast(I32)
        w2_woven = keep.tile([P, PACK * N], BF16, align_bytes=64)
        w2_codes = keep.tile([P, N], U32, align_bytes=64)
        w2_scales = keep.tile([P, N], U8, align_bytes=64)

        z_woven, z_codes, z_scales = {}, {}, {}
        for c in chunks:
            for kind in (U0, UX, UXX, UT):
                name = f"{kind}{c}"
                z_woven[kind, c] = keep.tile(
                    [P, PACK * CHUNK], BF16, align_bytes=64, name=f"woven_{name}", tag=f"woven_{name}"
                )
                z_codes[kind, c] = keep.tile([P, CHUNK], U32, align_bytes=64, name=f"codes_{name}")
                z_scales[kind, c] = keep.tile([P, CHUNK], U8, align_bytes=64, name=f"scales_{name}")

        pre, h, h_squared, slotted, banks, running, y_woven = {}, {}, {}, {}, {}, {}, {}

        def product(out, codes, scales, t, moving_codes, moving_scales):
            nc.tensor.matmul_mx(
                out,
                lhsT=codes[:, t * P : (t + 1) * P].bitcast(FP8X4),
                lhsT_scale=scales[:, t * P : (t + 1) * P],
                rhs=moving_codes.bitcast(FP8X4),
                rhs_scale=moving_scales,
                start=True,
                stop=True,
            )

        def first_layer(c):
            for pair in range(2):
                pre[c, pair] = psum.tile([P, 2, CHUNK], F32, name="bank")
                for e in range(2):
                    product(pre[c, pair][:, e, :], w1_codes, w1_scales, 2 * pair + e, x_codes[c][:], x_bytes[c][:])

        def tanh(c):
            h[c] = keep.tile([P, PACK, CHUNK], F32, name=f"h{c}")
            for pair in range(2):
                nc.scalar.activation(h[c][:, 2 * pair : 2 * pair + 2, :], pre[c, pair][:], ACT.Tanh)

        def square(c):
            h_squared[c] = keep.tile([P, PACK, CHUNK], F32, name=f"h_squared{c}")
            for pair in range(2):
                slots = slice(2 * pair, 2 * pair + 2)
                nc.scalar.activation(h_squared[c][:, slots, :], h[c][:, slots, :], ACT.Square)

        def new_slotted(kind, c, tag):
            slotted[kind, c] = keep.tile([P, PACK, CHUNK], F32, name=f"{kind}{c}", tag=tag, align_bytes=64)
            return slotted[kind, c]

        def slope(kind, c):
            row = (UX, UT).index(kind)
            z = new_slotted(kind, c, f"{kind}{c}")
            for t in range(PACK):
                nc.scalar.activation(
                    z[:, t, :], h_squared[c][:, t, :], ACT.Identity,
                    bias=gains[:, row, t : t + 1], scale=neg_gains[:, row, t : t + 1],
                )

        def hx_on_scalar(c):
            hx = new_slotted(HX, c, f"{HX}{c}")
            for t in range(PACK):
                nc.scalar.activation(hx[:, t, :], h[c][:, t, :], ACT.Copy, scale=minus_2wx[:, t : t + 1])

        def hx_on_gpsimd(c, tag):
            hx = new_slotted(HX, c, tag)
            for t in range(PACK):
                nc.gpsimd.tensor_scalar(hx[:, t, :], h[c][:, t, :], minus_2wx[:, t : t + 1], zero[:], MULT, ADD)

        def weave(kind, c, engine_copy):
            engine_copy(woven_walk(z_woven[kind, c][:]), slotted_walk(slotted[kind, c][:]))

        def woven_u0(c):
            spread = unit_c.unsqueeze(1).unsqueeze(3).to_broadcast([P, CHUNK // 2, PACK, 2])
            nc.vector.tensor_tensor(woven_walk(z_woven[U0, c][:]), slotted_walk(h[c][:]), spread, MULT)

        def woven_uxx(c):
            nc.vector.tensor_tensor(
                woven_walk(z_woven[UXX, c][:]),
                slotted_walk(slotted[HX, c][:]),
                slotted_walk(slotted[UX, c][:]),
                MULT,
            )

        def heads(kind, c):
            codes, scales = z_codes[kind, c], z_scales[kind, c]
            nc.vector.quantize_mx(codes[:].bitcast(FP8X4), scales[:], z_woven[kind, c][:])
            for n in range(2):
                bank = psum.tile([P, PACK, UNIT], F32, name="bank")
                cols = slice(n * UNIT, (n + 1) * UNIT)
                for t in range(PACK):
                    product(bank[:, t, :], w2_codes, w2_scales, t, codes[:, cols], scales[:, cols])
                banks[kind, 2 * c + n] = bank

        def units(c):
            return (2 * c, 2 * c + 1)

        def fetch_u0(c):
            for u in units(c):
                running[u] = work.tile([P, PACK, UNIT], F32, name="u0_sb")
                nc.scalar.copy(running[u][:], banks[U0, u][:])

        def times_ux(c):
            for u in units(c):
                prod = work.tile([P, PACK, UNIT], F32, name="prod")
                nc.vector.tensor_tensor(prod[:], banks[UX, u][:], running[u][:], MULT)
                running[u] = prod

        def minus_uxx(c):
            for u in units(c):
                part = work.tile([P, PACK, UNIT], F32, name="part")
                nc.vector.scalar_tensor_tensor(
                    flat(part[:]), flat(banks[UXX, u][:]), -0.3, flat(running[u][:]), MULT, ADD
                )
                running[u] = part

        def plus_ut(c):
            for u in units(c):
                y = keep.tile([P, PACK, UNIT], F32, name=f"y{u}")
                nc.vector.tensor_tensor(y[:], banks[UT, u][:], running[u][:], ADD)
                nc.sync.dma_start(out_rows[:, :, u * UNIT : (u + 1) * UNIT], y[:])
                running[u] = y

        def round_y(c, engine_copies):
            y_woven[c] = keep.tile([P, 2, PACK * UNIT], BF16, align_bytes=64, name=f"y_woven{c}")
            for n, u in enumerate(units(c)):
                engine_copies[n](woven_walk(y_woven[c][:, n, :]), slotted_walk(running[u][:]))

        def pack_y(c):
            cols = slice(c * CHUNK, (c + 1) * CHUNK)
            nc.vector.quantize_mx(
                y_codes[:, cols].bitcast(FP8X4), y_scales[:, cols], y_woven[c][:].rearrange("p n c -> p (n c)")
            )
            nc.sync.dma_start(out_words[:, cols], y_codes[:, cols].bitcast(I32))

        on_vector, on_scalar = nc.vector.tensor_copy, nc.scalar.copy

        first_layer(0)
        tanh(0)
        square(0)
        first_layer(1)
        for half in range(2):
            deal_weight(on_vector, w2_woven[:], weight_walk(w2_raw[half][:]), half * P // 2, P // 2)
        woven_u0(0)
        slope(UX, 0)
        hx_on_scalar(0)
        tanh(1)
        slope(UT, 0)
        nc.vector.quantize_mx(w2_codes[:].bitcast(FP8X4), w2_scales[:], w2_woven[:])
        heads(U0, 0)
        weave(UX, 0, on_vector)
        fetch_u0(0)
        square(1)
        heads(UX, 0)
        woven_uxx(0)
        woven_u0(1)
        heads(UXX, 0)
        weave(UT, 0, on_vector)
        heads(U0, 1)
        heads(UT, 0)

        slope(UX, 1)
        hx_on_gpsimd(1, f"woven_{UT}0")
        weave(UX, 1, on_scalar)
        fetch_u0(1)
        slope(UT, 1)
        weave(UT, 1, on_scalar)
        times_ux(0)
        minus_uxx(0)
        plus_ut(0)

        heads(UX, 1)
        woven_uxx(1)
        heads(UXX, 1)
        times_ux(1)
        heads(UT, 1)
        round_y(0, (on_scalar, on_scalar))
        minus_uxx(1)
        pack_y(0)
        plus_ut(1)
        round_y(1, (on_scalar, on_vector))
        pack_y(1)

        for q in range(QUADRANTS):
            queue = nc.sync if q % 2 == 0 else nc.scalar
            queue.dma_start(
                out_2[0, 4 * q : 4 * q + 4, :].bitcast(I32),
                y_scales[32 * q : 32 * q + 4, :].bitcast(I32),
            )
